import numpy as np, ml_dtypes
CORES = [5,29,101,125,133,157,229,253]
N = 8
BF = ml_dtypes.bfloat16
def gentries(a):
    return np.ascontiguousarray(a.reshape(8, 16, -1).transpose(0, 2, 1)).reshape(8, -1)
def gtable(e):
    e = np.asarray(e); return np.ascontiguousarray(e.reshape(8, -1, 16).transpose(0, 2, 1)).reshape(128, -1).astype(np.int32)
W, C, M, LO, SH, RO = 4096, 128, 32, 8, 6, 4
def parts(rng):
    return rng.integers(0, 256, (N, 8, 16, W)), rng.integers(0, W, (N, 8, C, M)), rng.integers(LO, M + 1, (N, 8, C)), rng.integers(1000, 1800, (N, 8, C))
def pack(bank, s, n, t):
    return {"bank": np.ascontiguousarray(bank.reshape(N, 128, W)).astype(np.float32).astype(BF), "arms": np.stack([gtable(a.transpose(0, 2, 1).reshape(8, -1)) for a in s]),
            "len0": np.stack([gtable(a) for a in n]), "th": np.stack([gtable(a) for a in t])}
def setup_inputs(rng):
    return pack(*parts(rng))
def setup_inputs_ties(rng):
    bank, s, n, t = parts(rng); pool = rng.integers(0, 256, (1, 8, 16, 3)); pool[:, 2, :, 0] = 0; pool[:, 2, :, 1:] = 255
    pick = rng.integers(0, 3, (N, 8, 1, W)); pick[0::2, 6] = 1
    pick[1::2, 6] = np.where(rng.random((N // 2, 1, W)) < 0.03, pick[1::2, 6], 1)
    bank = np.take_along_axis(np.repeat(pool, N, axis=0), pick, 3)
    far = np.add.reduce(np.abs(pool[0][:, :, :, None] - pool[0][:, :, None, :]), axis=1)
    i = rng.integers(0, 3, (N, 8, C)); j = rng.integers(0, 3, (N, 8, C))
    n[:, 4] = M; z = np.add.accumulate(s[:, 4], axis=2) & (W - 1); h = (((z * z) >> SH) + s[:, 4]) & (W - 1)
    c = np.arange(C); bank[:, 4] = pool[:, 4, :, :1]
    bank[np.arange(N)[:, None], 4, 0, h[:, c, M - 1 - c % 2]] = pool[0, 4, 0, 0] ^ 1
    return pack(bank, s, n, far[np.arange(8)[None, :, None], i, j] + rng.integers(0, 2, (N, 8, C)))
def setup_inputs_ends(rng):
    bank, s, n, t = parts(rng); e = rng.integers(0, W, (3, C))
    bank[:, 5] = bank[0, 5].copy(); bank[0::2, 7][:, :, e[1]] = 0; bank[1::2, 7][:, :, e[1]] = 255
    u = (rng.random((N, 16, C)) * rng.integers(1, 56, C)).astype(np.int64)
    bank[0::2, 6][:, :, e[2]] = u[0::2]; bank[1::2, 6][:, :, e[2]] = 255 - u[1::2]
    np.put_along_axis(s[:, 5], n[:, 5, :, None] - 1, e[0][None, :, None], 2)
    np.put_along_axis(s[:, 6], n[:, 6, :, None] - 1, e[2][None, :, None], 2)
    np.put_along_axis(s[:, 7], n[:, 7, :, None] - 1, e[1][None, :, None], 2)
    last = np.take_along_axis(s, n[..., None] - 1, 3)[..., 0]; end = np.take_along_axis(bank, last[:, :, None, :], 3)
    t = np.add.reduce(np.abs(end - np.roll(end, 1, axis=0)), axis=2) + rng.integers(0, 2, (N, 8, C))
    t[:, 0] = 0; t[:, 1] = 4081
    return pack(bank, s, n, t)
def setup_inputs_lengths(rng):
    bank, s, n, t = parts(rng)
    n[:, 0] = LO; n[:, 1] = M
    x = rng.integers(LO + 1, M - LO, C); n[:, 2] = x
    n[1::2, 2] = M - x + rng.integers(-1, 2, (N // 2, C)); t[:, 2] = 4081
    n[:, 3] = M // 2 + rng.integers(-1, 2, (N, C)); t[:, 3] = 0
    n[:, 4] = rng.choice(np.array([LO, LO + 1, M - 1, M]), (N, C)); t[:, 4] = rng.choice(np.array([0, 4081]), (N, C))
    return pack(bank, s, n, t)
def setup_inputs_codes(rng):
    bank, s, n, t = parts(rng)
    s[:, 0] = W - 1; n[:, 0] = np.maximum(n[:, 0], rng.integers(LO, M + 1, (N, C))); n[:, 0, :4] = M
    bank[:, 0] = rng.integers(128, 256, (N, 16, W)); t[:, 0] = rng.integers(500, 900, (N, C))
    z = (M * (W - 1) - 1) & (W - 1); bank[:, 0, :, (((z * z) >> SH) + W - 1) & (W - 1)] = 0
    s[:, 1] = 0; s[:, 2] = s[:, 2] & (W - 2); s[:, 3] = s[:, 3] | 1
    s[:, 4] = s[:, 4, :, :1].copy(); s[:, 6] = rng.choice(np.array([0, 1, W - 2, W - 1]), (N, C, M))
    s[:, 5, :, LO - 1:] = 0; n[:, 5] = M
    s[:, 7] = rng.integers(W - 16, W, (N, C, M)); bank[:, 7] = rng.integers(192, 256, (N, 16, W)); t[:, 7] = rng.integers(250, 450, (N, C))
    bank[:, 7][:, :, (((W - 1) * (W - 1) >> SH) + np.arange(W - 16, W)) & (W - 1)] = 0
    return pack(bank, s, n, t)
def setup_inputs_spread(rng):
    bank, s, n, t = parts(rng)
    bank = np.minimum((np.exp2(rng.integers(0, 9, (N, 8, 1, W))) * rng.random((N, 8, 16, W))).astype(np.int64), 255)
    s = (W * rng.random((N, 8, C, M)) ** rng.choice(np.array([1, 2, 5]), (N, 8, C, 1))).astype(np.int64)
    n = np.minimum(LO + ((M + 1 - LO) * rng.random((N, 8, C)) ** rng.choice(np.array([1, 3]), (N, 8, 1))).astype(np.int64), M)
    t = np.minimum(np.exp2(12 * rng.random((N, 8, C))).astype(np.int64), 4081)
    return pack(bank, s, n, t)
def check_inputs(d):
    bad = []; v = np.asarray(d["bank"]).astype(np.float32)
    if not np.all((v >= 0) & (v <= 255) & (v == np.floor(v))): bad.append("bank holds whole numbers from 0 to 255")
    for k, lo, hi in (("arms", 0, W - 1), ("len0", LO, M), ("th", 0, 4081)):
        if np.min(d[k]) < lo or np.max(d[k]) > hi: bad.append("range of " + k)
    return bad
def reference(bank, arms, len0, th):
    B = bank.astype(np.float32).astype(np.int32).reshape(N, 8, 16, W)
    S = np.stack([gentries(a) for a in arms]).astype(np.int64).reshape(N, 8, M, C).transpose(0, 1, 3, 2)
    n = np.stack([gentries(a) for a in len0]).astype(np.int64); T = np.stack([gentries(a) for a in th]).astype(np.int64)
    A = np.zeros((N, 8, C), np.int64); k = np.arange(M)
    for t in range(RO):
        d = 1 + t % (N - 1)
        last = np.take_along_axis(S, n[..., None] - 1, 3)[..., 0]
        E = np.take_along_axis(B, last[:, :, None, :], 3)
        near = np.add.reduce(np.abs(E - np.roll(E, d, axis=0)), axis=2) < T
        S2 = np.where(near[..., None], np.roll(S, d, axis=0), S); n2 = np.where(near, np.roll(n, d, axis=0), n)
        L = np.minimum(n + n2, M)
        back = np.clip((n + n2)[..., None] - 1 - k, 0, M - 1)
        Q = np.where(k < n[..., None], S, np.take_along_axis(S2, back, 3) ^ 1)
        Q = np.where(k < L[..., None], Q, 0)
        z = (np.add.accumulate(Q, axis=3) + A[..., None]) & (W - 1)
        h = (((z * z) >> SH) + Q) & (W - 1)
        R = np.take_along_axis(B, h.reshape(N, 8, 1, C * M), 3).reshape(N, 8, 16, C, M)
        D = np.add.reduce(np.abs(R[..., 1:] - R[..., :-1]), axis=2)
        ok = (k[1:] >= LO) & (k[1:] < L[..., None])
        b = 1 + np.argmax(np.where(ok, D, -1), axis=3)
        A = A + np.take_along_axis(np.add.reduce(R, axis=2), b[..., None], 3)[..., 0]
        S = np.where(k < b[..., None], Q, 0); n = b
    ys = np.stack([gtable(a.transpose(0, 2, 1).reshape(8, -1)) for a in S]).astype(np.float32)
    yn = np.stack([gtable(a) for a in n]).astype(np.float32); ya = np.stack([gtable(a) for a in A]).astype(np.float32)
    return {"ys": ys, "yn": yn, "ya": ya}

import numpy as np
from concourse.mybir import AluOpType as ALU, ActivationFunctionType as AF, AxisListType as AX

RO, NB = 4, 2
XV = False
V_BANK = (1, 3)
WD = 832 if XV else 64
F, I32, BF, U16 = "float32", "int32", "bfloat16", "uint16"
SCRATCH = {
    "bk": ("sbuf", [128, 4096], BF), "ar": ("sbuf", [128, 256], I32), "ln": ("sbuf", [128, 8], I32),
    "ti": ("sbuf", [128, 8], I32), "tf": ("sbuf", [128, 8], F),
    "pi": ("sbuf", [128, 8], I32), "pf": ("sbuf", [128, 8], F),
    "x": ("sbuf", [128, 144], F), "c16": ("sbuf", [128, WD], F), "s26": ("sbuf", [128, 130], F),
    "iv": ("sbuf", [128, 130], F), "js": ("sbuf", [128, 65], F), "ncc": ("sbuf", [128, 8], F),
    "idf": ("sbuf", [128, 128], F), "idb": ("sbuf", [128, 384], BF), "b1": ("sbuf", [128, 144], BF),
    "b256": ("sbuf", [128, 144], BF), "mk": ("sbuf", [128, 2048], F), "dm": ("sbuf", [128, WD], F),
    "rs16": ("sbuf", [128, WD], F), "rs26": ("sbuf", [128, 112], F), "d0k": ("sbuf", [128, 112], F),
    "gv": ("sbuf", [128, 112], F), "tmp": ("sbuf", [128, 112], F), "kc": ("sbuf", [128, 112], BF),
    "lf": ("sbuf", [128, 8], F), "li": ("sbuf", [128, 8], I32), "lu": ("sbuf", [128, 8], U16),
    "sf": ("sbuf", [128, 272], F), "s4": ("sbuf", [128, 264], F), "sg": ("sbuf", [128, 272], F),
    "oys": ("sbuf", [128, 256], F), "oyn": ("sbuf", [128, 8], F), "oya": ("sbuf", [128, 8], F),
}
for _b in range(NB):
    for _n, _w, _d in (("Q", 104, F), ("H", 104, I32), ("U", 112, U16), ("R", 1664, BF), ("AD", 1664, BF),
                       ("JW", 832, F), ("JS", WD, F), ("ju", 64, U16), ("yi", 64, I32), ("G", 104, F),
                       ("M", 104, I32), ("rr", 104, F), ("zz", 104, F), ("Qb", 104, F),
                       ("hi", 104, I32), ("T4", 104, F), ("RM", 104, F), ("sm", 64, F), ("si", 16, I32),
                       ("su", 16, U16), ("sel", 64, F), ("ssc", 64, F), ("inv", 112, BF), ("ge", 112, F)):
        SCRATCH["%s%d" % (_n, _b)] = ("sbuf", [128, _w], _d)
    for _t in range(RO):
        SCRATCH["win%d%d" % (_t, _b)] = ("sbuf", [128, 296], F)
        SCRATCH["land%d%d" % (_t, _b)] = ("sbuf", [128, 72], BF)
    for _t in range(RO + 1):
        SCRATCH["msg%d%d" % (_t, _b)] = ("sbuf", [128, 200], BF)
    for _n in ("X", "K", "D0", "D1"):
        SCRATCH["p%s%d" % (_n, _b)] = ("psum", [128, 512], F)
SEMAPHORES = ["V", "A", "P", "G", "d_ar", "d_ln", "d_th", "d_bk", "d_ys", "d_yn", "d_ya", "sent", "aK00", "aK01"] + \
    ["%s%d%d" % (k, t, b) for k in ("aY", "aE") for t in range(RO) for b in range(NB)]

MAGIC = 1.5 * 2.0 ** 35
EVEN, DOWN = 1.5 * 2.0 ** 24, 1.0 - 2.0 ** -13
BIG = 2.0 ** 21
CY, PCY, GC, LAT, HOP = 1.0, 0.5, 1.56, 90.0, 2200.0
BIAS, TRIES = 4000.0, 500


def build():
    ops = []
    cur = [None]

    def op(eng, fn, r, w, cost, lat=0.0, sem=None, after=None):
        ops.append({"e": eng, "f": fn, "r": r, "w": w, "c": cost, "l": lat, "s": sem, "b": cur[0], "a": after})
        return len(ops) - 1

    def V(fn, r, w, n, ind=False):
        op("V", lambda g, T, c: fn(g.vector, T), r, w, (60 + n * GC * CY) if ind else 20 + max(64, n) * CY)

    def A(fn, r, w, n, ind=False):
        op("A", lambda g, T, c: fn(g.scalar, T), r, w, (75 + n * GC * CY) if ind else 20 + max(64, n) * CY)

    def P(fn, r, w, n):
        op("P", lambda g, T, c: fn(g.tensor, T), r, w, 20 + n * PCY)

    def iota(name, n, pat, base):
        op("G", lambda g, T, c: g.iota(T[name][:, 0:n], pat, base, 0, allow_small_or_imprecise_dtypes=True), [], [name], 150 + 2 * n * CY)

    def val(s, T):
        return s if isinstance(s, (int, float)) else s(T)

    def ts(out, in0, s1, s2, o0, o1, r, w, n):
        if o1 is None:
            V(lambda v, T: v.tensor_scalar(out(T), in0(T), val(s1, T), None, o0), r, w, n)
        else:
            V(lambda v, T: v.tensor_scalar(out(T), in0(T), val(s1, T), val(s2, T), o0, o1), r, w, n)

    def tt(out, a, b, o, r, w, n, ind=False):
        V(lambda v, T: v.tensor_tensor(out(T), a(T), b(T), o), r, w, n, ind)

    def cp(out, a, r, w, n, ind=False):
        V(lambda v, T: v.tensor_copy(out(T), a(T)), r, w, n, ind)

    def scan(out, a, b, o0, o1, r, w, n):
        V(lambda v, T: v.tensor_tensor_scan(out(T), a(T), b(T), 0.0, o0, o1), r, w, n)

    def fill(out, c, w, n):
        V(lambda v, T: v.memset(out(T), c), [], w, n)

    def act(out, a, fn, r, w, n, ind=False, scale=None, bias=None):
        def f(s, T):
            k = {}
            if scale is not None:
                k["scale"] = val(scale, T)
            if bias is not None:
                k["bias"] = val(bias, T)
            return s.activation(out(T), a(T), fn, **k)
        A(f, r, w, n, ind)

    def ap(name, a=None, b=None, s=None):
        return lambda T: T[name][:, slice(a, b, s)]

    def ind(name, a, b, lst, c0, c1):
        return lambda T: T[name][:, a:b].indirect(T[lst][:, c0:c1])

    def send(kind, t, b, src, r, nbytes):
        name = "%s%d%d" % (kind, t, b)
        i = op("G", lambda g, T, c: c["send"](t, name, src(T), piece(T, name)), r, [], 300, sem="sent")
        op("N", None, [], [name], 0, lat=(HOP + nbytes / 60.0) * (1.8 if t % 2 == 0 else 1.0), sem=name, after=i)

    op("S", lambda g, T, c: g.sync.dma_start(T.ar[:], T.arms[:]), [], ["ar"], 100, 2300, "d_ar")
    op("A", lambda g, T, c: g.scalar.dma_start(T.bk[:], T.bank[:]), [], ["bk"], 100, 6000, "d_bk")
    op("S", lambda g, T, c: g.sync.dma_start(T.ln[:], T.len0[:]), [], ["ln"], 100, 2200, "d_ln")
    op("S", lambda g, T, c: g.sync.dma_start(T.ti[:], T.th[:]), [], ["ti"], 100, 2200, "d_th")
    op("G", lambda g, T, c: g.iota(T.pi[:, 0:1], [[0, 1]], 0, 1), [], ["pi"], 152)
    iota("c16", WD, [[0, WD // 16], [1, 16]], 0)
    iota("ncc", 4, [[-26, 4]], 262)
    iota("x", 144, [[1, 144]], 0)
    iota("s26", 130, [[0, 5], [1, 26]], 0)
    iota("js", 65, [[-20, 5], [-2, 13]], 517)
    iota("iv", 130, [[52, 5], [1, 26]], -517)
    ts(ap("pi", 1, 2), ap("pi", 0, 1), 15, None, ALU.bitwise_and, None, ["pi"], ["pi1"], 1)
    cp(ap("pf", 0, 2), ap("pi", 0, 2), ["pi", "pi1"], ["pf"], 2)
    tt(ap("pf", 3, 4), ap("pf", 0, 1), ap("pf", 1, 2), ALU.subtract, ["pf"], ["pf3"], 1)
    ts(ap("pf", 2, 3), ap("pf", 3, 4), 15.0, None, ALU.add, None, ["pf3"], ["pf2"], 1)
    ts(ap("pf", 4, 5), ap("pf", 1, 2), 4096.0, None, ALU.add, None, ["pf"], ["pf4"], 1)
    ts(ap("dm"), ap("c16"), ap("pf", 1, 2), None, ALU.is_equal, None, ["c16", "pf"], ["dm"], WD)
    ts(ap("rs16"), ap("c16"), 0.0, None, ALU.not_equal, None, ["c16"], ["rs16"], WD)
    ts(ap("idf"), ap("x", 0, 128), ap("pf", 0, 1), None, ALU.is_equal, None, ["x", "pf"], ["idf"], 128)
    for k, sc in enumerate((1.0, -1.0, -BIG)):
        act(ap("idb", 128 * k, 128 * k + 128), ap("idf"), AF.Copy, ["idf"], ["idb%d" % k], 128, scale=sc)
    for r in range(0 if XV else 16):
        act(ap("mk", 128 * r, 128 * r + 128), ap("idf"), AF.Copy, ["idf", "dm"], ["mk%d" % r], 128, scale=ap("dm", r, r + 1))
    MK = ["mk%d" % r for r in range(16)]
    ts(ap("b1"), ap("x"), ap("pf", 2, 3), None, ALU.is_equal, None, ["x", "pf2"], ["b1"], 144)
    ts(ap("b256"), ap("x"), ap("pf", 2, 3), 256.0, ALU.is_equal, ALU.mult, ["x", "pf2"], ["b256"], 144)
    ts(ap("rs26"), ap("s26", 0, 112), 0.0, None, ALU.not_equal, None, ["s26"], ["rs26"], 112)
    ts(ap("d0k"), ap("s26", 0, 112), 0.0, -2.0 * BIG, ALU.is_equal, ALU.mult, ["s26"], ["d0k"], 112)
    ts(ap("tmp"), ap("s26", 0, 112), 2.0, 1024.0, ALU.is_lt, ALU.mult, ["s26"], ["tmp"], 112)
    ts(ap("s4", 0, 112), ap("x", 0, 112), -1.0, 256.0, ALU.mult, ALU.add, ["x"], ["s4"], 112)
    tt(ap("gv"), ap("s4", 0, 112), ap("tmp"), ALU.add, ["s4", "tmp"], ["gv"], 224)
    ts(ap("tmp"), ap("tmp"), -2048.0, None, ALU.mult, None, ["tmp"], ["tmp"], 112)
    tt(ap("kc"), ap("s4", 0, 112), ap("tmp"), ALU.add, ["s4", "tmp"], ["kc"], 224)
    ts(ap("lf"), ap("x", 0, 128, 16), ap("pf", 1, 2), None, ALU.add, None, ["x", "pf"], ["lf"], 8)
    ts(ap("li"), ap("lf"), 1.0 / 26, -0.48, ALU.mult, ALU.add, ["lf"], ["li"], 8)
    cp(ap("lu"), ap("li"), ["li"], ["lu"], 8)
    cp(ap("tf"), ap("ti"), ["ti"], ["tf"], 8)
    cp(ap("oys", 0, 56), ap("ar", 0, 56), ["ar"], ["oysA"], 56)
    fill(ap("sf", 0, 8), 0.0, ["sfp"], 8)
    fill(ap("sf", 264, 272), 0.0, ["sfp"], 8)
    for cc in range(8):
        cp(ap("sf", 8 + 32 * cc, 40 + 32 * cc), ap("ar", cc, 256, 8), ["ar"], ["sf%d" % cc], 32)
    SF = ["sfp"] + ["sf%d" % cc for cc in range(8)]
    act(ap("sg"), ap("sf"), AF.Identity, SF, ["sg"], 272, bias=EVEN, scale=DOWN)
    act(ap("sg"), ap("sg"), AF.Identity, ["sg"], ["sg"], 272, bias=-2.0 * EVEN, scale=2.0)
    tt(ap("sg"), ap("sg"), ap("sf"), ALU.subtract, SF + ["sg"], ["sg"], 544)
    act(ap("s4"), ap("sg", 7, 271), AF.Identity, ["sg"], ["s4"], 264, bias=4097.0, scale=4096.0)

    def batch(b):
        cur[0] = b
        B = str(b)
        Q, H, U, R, AD, JW, T4, GG = "Q" + B, "H" + B, "U" + B, "R" + B, "AD" + B, "JW" + B, "T4" + B, "G" + B
        sm, si, su, yi, ju = "sm" + B, "si" + B, "su" + B, "yi" + B, "ju" + B
        pX, pK, pD = "pX" + B, "pK" + B, ["pD0" + B, "pD1" + B]
        n2, dn, near, t1, b0 = ap(sm, 0, 4), ap(sm, 8, 12), ap(sm, 16, 20), ap(sm, 24, 28), ap(sm, 56, 60)
        mm, kb, mxi, qp = ap(sm, 32, 36), ap(si, 0, 4), ap(si, 8, 12), ap(pD[1], 384, 488)
        fill(ap(sm), 0.0, [x + B for x in ("n2", "dn", "near", "t1", "b0", "mm", "m0")], 64)
        fill(ap(si), 0, ["kb" + B, "mxi" + B], 16)
        for cc in range(4):
            fill(ap(AD, 416 * cc, 416 * cc + 32), 0.0, [AD + "z%d" % cc], 32)
            fill(ap(R, 416 * cc, 416 * cc + 16), 0.0, [R + str(cc)], 16)
        for t in range(RO):
            fill(ap("win%d%d" % (t, b), 272, 296), 0.0, ["wp%d%d" % (t, b)], 24)
        w0 = "win0" + B
        tt(ap(w0, 0, 136), ap("sg", 8 + 128 * b, 144 + 128 * b), ap("s4", 128 * b, 128 * b + 136), ALU.add, ["sg", "s4"], [w0], 272)
        send("aY", 0, b, ap(w0, 0, 136), [w0], 69632)
        for t in range(1, RO):
            act(ap("win%d%d" % (t, b), 0, 136), ap(w0, 0, 136), AF.Copy, [w0], ["win%d%d" % (t, b)], 136)
        for cc in range(4):
            o = 8 + 32 * (4 * b + cc)
            act(ap(Q, 26 * cc + 1, 26 * cc + 26), ap("sf", o + 7, o + 32), AF.Copy, SF, [Q + "c%d" % cc], 25)
            V(lambda v, T, cc=cc, o=o: v.tensor_reduce(T[sm][:, 24 + cc:25 + cc], T.sf[:, o:o + 7], AX.X, ALU.add), SF, ["t1" + B], 7)
        ts(b0, t1, -2047.5, None, ALU.add, None, ["t1" + B], ["b0" + B], 4)
        cp(ap(Q, 0, 104, 26), b0, ["b0" + B] + [Q + "c%d" % cc for cc in range(4)], [Q], 4)
        tt(kb, ap("ncc", 0, 4), ap("ln", 4 * b, 4 * b + 4), ALU.subtract, ["ncc", "ln"], ["kb" + B], 4)

        def ends(t):
            msg = "msg%d%d" % (t, b)
            if t > 0:
                ts(ap(su, 12, 16), kb, -16.0, ap("pf", 4, 5), ALU.mult, ALU.add, ["kb" + B, "pf4"], ["ro" + B], 4)
                act(ap(msg, 72, 136), ind(R, 0, 1664, su, 12, 16), AF.Copy, [R + str(cc) for cc in range(4)] + ["ro" + B], [msg + "r"], 64, True)
            if t < RO:
                ts(ap(su, 0, 4), kb, -1.0, 255.0, ALU.mult, ALU.add, ["kb" + B], ["off" + B], 4)
                tt(ap("sel" + B), ind(Q, 0, 104, su, 0, 4), ap("dm", 0, 64), ALU.mult, [Q, "off" + B, "dm"], ["sel" + B], 64, True)
                scan(ap("ssc" + B), ap("rs16", 0, 64), ap("sel" + B), ALU.mult, ALU.add, ["sel" + B, "rs16"], ["ssc" + B], 64)
                cp(ap(su, 8, 12), ap("ssc" + B, 15, 64, 16), ["ssc" + B], ["el" + B], 8)
                cp(ap(msg, 8, 72), ind("bk", 0, 4096, su, 8, 12), ["bk", "el" + B], [msg], 64, True)
                ts(ap(msg, 4, 8), kb, -136.0, None, ALU.add, None, ["kb" + B], [msg + "k"], 4)
                if t == 0:
                    send("aK", t, b, ap(msg, 4, 8), [msg + "k"], 1024)
                    send("aE", t, b, ap(msg, 8, 72), [msg], 16384)
                else:
                    send("aE", t, b, ap(msg, 4, 72), [msg, msg + "k"], 17408)
                act(n2, ap(msg, 4, 8), AF.Identity, [msg + "k"], ["n2" + B], 4, bias=-272.0, scale=-2.0)
                act(qp, ap(Q), AF.Copy, [Q], ["@" + pD[1], "Qp" + B], 104)
            tt(ap("ge" + B), ind(si, 0, 8, "lu", 0, 7), ap("gv"), ALU.is_ge if t < RO else ALU.is_lt, ["kb" + B, "lu", "gv"], ["ge" + B], 112, True)

        def sums(t):
            msg = "msg%d%d" % (t, b)
            c0, c1 = (72 if t > 0 else 136), (200 if t < RO else 136)
            o0 = (c0 - 72) // 16

            def f(p, T):
                for r in range(16):
                    x = p.matmul(T[pX][:, o0:o0 + (c1 - c0) // 16], T.b1[:, 15 - r:143 - r], T[msg][:, c0 + r:c1:16], r == 0, r == 15)
                return x
            P(f, [msg + "r", msg + "d", "b1"], ["@" + pX, "dist" + B], 1024)

        def rnd(t):
            msg, land, win = "msg%d%d" % (t, b), "land%d%d" % (t, b), "win%d%d" % (t, b)
            aE, aY = "aE%d%d" % (t, b), "aY%d%d" % (t, b)

            def fe(p, T):
                p.matmul(T[pD[0]][:, 0:64], T.idb[:, 0:128], T[msg][:, 8:72], True, False)
                return p.matmul(T[pD[0]][:, 0:64], T.idb[:, 128:256], T[land][:, 4:68], False, True)
            P(fe, [msg, aE, "idb0", "idb1"], ["@" + pD[0], "dE" + B], 128)
            act(ap(msg, 136, 200), ap(pD[0], 0, 64), AF.Abs, ["dE" + B], ["@" + pD[0], msg + "d"], 64)
            sums(t)
            tt(dn, kb, ap(land, 0, 4), ALU.subtract, ["kb" + B, aE if t else "aK0" + B], ["dn" + B], 4)
            tt(near, ap(pX, 4, 8), ap("tf", 4 * b, 4 * b + 4), ALU.is_lt, ["dist" + B, "tf"], ["@" + pX, "near" + B], 4)
            tt(t1, near, dn, ALU.mult, ["near" + B, "dn" + B], ["t1" + B], 4)
            for cc in range(4):
                ts(ap(ju, 13 * cc, 13 * cc + 13), ap("js", 13 * cc, 13 * cc + 13), ap(sm, 24 + cc, 25 + cc), ap(sm, cc, cc + 1), ALU.add, ALU.add,
                   ["t1" + B, "n2" + B, "js"], [ju + str(cc // 2)], 13)
            if t > 0:
                tt(ap(Q, 0, 104, 26), ap(pX, 0, 4), ap(Q, 0, 104, 26), ALU.add, ["dist" + B, Q], ["@" + pX, Q], 4)
            rd = [win, aY, "wp%d%d" % (t, b)]
            if XV:
                tt(ap(JW), ind(win, 0, 296, ju, 0, 52), ap("dm"), ALU.mult, rd + ["dm", ju + "0", ju + "1"], [JW], 832, True)
                scan(ap("JS" + B), ap("rs16"), ap(JW), ALU.mult, ALU.add, [JW, "rs16"], ["y" + B], 832)
                cp(ap(yi, 0, 52), ap("JS" + B, 15, 832, 16), ["y" + B], [yi], 52)
            else:
                act(ap(JW, 0, 416), ind(win, 0, 296, ju, 0, 26), AF.Copy, rd + [ju + "0"], [JW + "a"], 416, True)
                cp(ap(JW, 416, 832), ind(win, 0, 296, ju, 26, 52), rd + [ju + "1"], [JW + "b"], 416, True)

                def fx(p, T):
                    for r in range(16):
                        x = p.matmul(T[pK][:, 0:52], T.mk[:, 128 * r:128 * r + 128], T[JW][:, r:832:16], r == 0, r == 15)
                    return x
                P(fx, [JW + "a", JW + "b"] + MK, ["@" + pK, "y" + B], 4096)
                cp(ap(yi, 0, 52), ap(pK, 0, 52), ["y" + B], ["@" + pK, yi], 52)
            act(mm, dn, AF.Identity, ["dn" + B], ["mm" + B], 4, bias=-136.0)
            for cc in range(4):
                act(ap(sm, 40 + cc, 41 + cc), ap(sm, 16 + cc, 17 + cc), AF.Identity, ["near" + B, "mm" + B, "n2" + B], ["m0" + B], 1,
                    scale=ap(sm, 32 + cc, 33 + cc), bias=ap(sm, cc, cc + 1))
            tt(ap("inv" + B), ind(sm, 40, 48, "lu", 0, 7), ap("iv", 0, 112), ALU.is_lt, ["m0" + B, "lu", "iv"], ["inv" + B], 112, True)
            ts(ap("M" + B, 0, 104, 2), ap(yi, 0, 52), 4095, None, ALU.bitwise_and, None, [yi], ["Ml" + B], 52)
            ts(ap("M" + B, 1, 104, 2), ap(yi, 0, 52), 12, None, ALU.logical_shift_right, None, [yi], ["Mh" + B], 52)
            tt(ap(pX, 128, 232), ap("M" + B), qp, ALU.subtract, ["Ml" + B, "Mh" + B, "Qp" + B], ["@" + pX, "@" + pD[1], "d" + B], 104)
            tt(ap(pX, 256, 360), ap(pX, 128, 232), ap("ge" + B, 0, 104), ALU.mult, ["d" + B, "ge" + B], ["@" + pX, "d2" + B], 104)
            tt(ap(Q), ap(pX, 256, 360), ap(Q), ALU.add, ["d2" + B, Q], ["@" + pX, Q], 104)
            scan(ap(pX, 384, 488), ap("rs26", 0, 104), ap(Q), ALU.mult, ALU.add, [Q, "rs26"], ["@" + pX, "p" + B], 104)
            act(ap("Qb" + B), ap(Q), AF.Identity, [Q], ["Qb" + B], 104, bias=-29.0 / 64)
            ts(ap("rr" + B), ap(pX, 384, 488), MAGIC, -MAGIC, ALU.add, ALU.add, ["p" + B], ["@" + pX, "rr" + B], 104)
            tt(ap("zz" + B), ap(pX, 384, 488), ap("rr" + B), ALU.subtract, ["p" + B, "rr" + B], ["@" + pX, "zz" + B], 104)
            act(ap(pK, 128, 232), ap("zz" + B), AF.Square, ["zz" + B], ["@" + pK, "sq" + B], 104, bias=2047.5 / 8, scale=0.125)
            tt(ap("hi" + B), ap(pK, 128, 232), ap("Qb" + B), ALU.add, ["sq" + B, "Qb" + B], ["@" + pK, "hi" + B], 104)
            ts(ap(H), ap("hi" + B), 4095, None, ALU.bitwise_and, None, ["hi" + B], [H], 104)
            cp(ap(U, 1, 105), ap(H), [H], [U], 104)
            if t + 1 < RO:
                wn = "win%d%d" % (t + 1, b)
                act(ap(T4), ap(Q), AF.Identity, [Q], [T4], 104, bias=EVEN, scale=DOWN)
                act(qp, ap(T4), AF.Identity, [T4], ["@" + pD[1], "Qp" + B], 104, bias=-2.0 * EVEN, scale=2.0)
                tt(ap(GG), qp, ap(Q), ALU.subtract, [Q, "Qp" + B], ["@" + pD[1], GG], 104)
                act(ap(T4), ap(GG), AF.Identity, [GG], [T4], 104, bias=4097.0, scale=4096.0)
                for cc in range(4):
                    tt(ap(wn, 32 * cc + 8, 32 * cc + 32), ap(GG, 26 * cc + 2, 26 * cc + 26), ap(T4, 26 * cc + 1, 26 * cc + 25), ALU.add, [GG, T4], [wn], 48)
                send("aY", t + 1, b, ap(wn, 0, 136), [wn], 69632)
            for cc in range(4):
                o, src = ap(R, 416 * cc + 16, 416 * cc + 416), ind("bk", 0, 4096, U, 26 * cc + 2, 26 * cc + 27)
                if cc in V_BANK:
                    cp(o, src, ["bk", U], [R + str(cc)], 400, True)
                else:
                    act(o, src, AF.Copy, ["bk", U], [R + str(cc)], 400, True)
            for cc in range(4):
                o, d = 416 * cc, pD[cc % 2]

                def fd(p, T, o=o, d=d):
                    p.matmul(T[d][:, 0:384], T.idb[:, 0:128], T[R][:, o + 32:o + 416], True, False)
                    return p.matmul(T[d][:, 0:384], T.idb[:, 128:256], T[R][:, o + 16:o + 400], False, True)
                P(fd, [R + str(cc), "idb0", "idb1"], ["@" + d, d], 768)
                act(ap(AD, o + 32, o + 416), ap(d, 0, 384), AF.Abs, [d], ["@" + d, AD + str(cc)], 384)
            for h in range(2):
                def fk(p, T, h=h):
                    out = T[pK][:, 256 + 52 * h:308 + 52 * h]
                    p.matmul(out, T.idb[:, 0:128], T.kc[:, 52 * h:52 * h + 52], True, False)
                    p.matmul(out, T.idb[:, 256:384], T["inv" + B][:, 52 * h:52 * h + 52], False, False)
                    for r in range(16):
                        x = p.matmul(out, T.b256[:, 15 - r:143 - r], T[AD][:, 832 * h + r:832 * h + 832:16], False, r == 15)
                    return x
                P(fk, ["kc", "idb0", "idb2", "inv" + B, "b256"] + [AD + y % cc for cc in (2 * h, 2 * h + 1) for y in ("%d", "z%d")],
                  ["@" + pK, "key" + B], 1152)
            scan(ap("RM" + B), ap("d0k", 0, 104), ap(pK, 256, 360), ALU.add, ALU.max, ["key" + B, "d0k"], ["@" + pK, "RM" + B], 104)
            cp(mxi, ap("RM" + B, 25, 104, 26), ["RM" + B], ["mxi" + B], 4)
            ts(kb, mxi, 255, None, ALU.bitwise_and, None, ["mxi" + B], ["kb" + B], 4)

        for t in range(RO):
            ends(t)
            rnd(t)
        ends(RO)
        sums(RO)
        tt(t1, ap(pX, 0, 4), ap(Q, 0, 104, 26), ALU.add, ["dist" + B, Q], ["@" + pX, "t1" + B], 4)
        tt(ap("oya", 4 * b, 4 * b + 4), t1, b0, ALU.subtract, ["t1" + B, "b0" + B], ["oya" + B], 4)
        tt(ap("oyn", 4 * b, 4 * b + 4), ap("ncc", 0, 4), kb, ALU.subtract, ["ncc", "kb" + B], ["oyn" + B], 4)
        for cc in range(4):
            tt(ap("oys", 56 + 4 * b + cc, 256, 8), ap(Q, 26 * cc + 1, 26 * cc + 26), ap("ge" + B, 26 * cc + 1, 26 * cc + 26), ALU.mult,
               [Q, "ge" + B], ["oys%d%d" % (b, cc)], 50)

    for b in range(NB):
        batch(b)
    cur[0] = None
    op("S", lambda g, T, c: g.sync.dma_start(T.ys[:], T.oys[:]), ["oysA"] + ["oys%d%d" % (b, cc) for b in range(NB) for cc in range(4)], [], 100, 2300, "d_ys")
    op("S", lambda g, T, c: g.sync.dma_start(T.yn[:], T.oyn[:]), ["oyn0", "oyn1"], [], 100, 2200, "d_yn")
    op("A", lambda g, T, c: g.scalar.dma_start(T.ya[:], T.oya[:]), ["oya0", "oya1"], [], 100, 2200, "d_ya")
    return ops


def plan(ops):
    n = len(ops)
    dep = [dict() for _ in range(n)]
    lastw, readers = {}, {}
    for i, o in enumerate(ops):
        def add(j, raw):
            same = ops[j]["e"] == o["e"] and ops[j]["s"] is None
            dep[i][j] = dep[i].get(j, False) or raw or not same
        for x in o["r"]:
            for j in lastw.get(x, []):
                add(j, True)
        for x in o["w"]:
            for j in lastw.get(x, []) + readers.get(x, []):
                if j != i:
                    add(j, False)
        for x in o["r"]:
            readers.setdefault(x, []).append(i)
        for x in o["w"]:
            keep = [j for j in lastw.get(x, []) if not readers.get(x) and x[0] != "@"]
            lastw[x] = keep + [i]
            readers[x] = []
        if o["a"] is not None:
            dep[i][o["a"]] = False
    succ = [[] for _ in range(n)]
    for i in range(n):
        for j in dep[i]:
            succ[j].append(i)
    pr = [0.0] * n
    for i in range(n - 1, -1, -1):
        early = 3000.0 if str(ops[i]["s"])[:3] in ("aY0", "aK0") else 0.0
        pr[i] = ops[i]["c"] + ops[i]["l"] + early + max([pr[k] + LAT for k in succ[i]] + [0.0])
    pr = np.array([pr[i] + (BIAS if ops[i]["b"] == 0 else 0.0) for i in range(n)])

    def place(p):
        left = [len(d) for d in dep]
        ready = [(-p[i], i) for i in range(n) if left[i] == 0]
        busy, start, fin = {}, [0.0] * n, [0.0] * n
        while ready:
            ready.sort()
            i = ready.pop(0)[1]
            o = ops[i]
            s = max([0.0] + [(fin[j] + LAT if w or o["e"] == "N" else start[j] + ops[j]["c"]) for j, w in dep[i].items()])
            if o["e"] != "N":
                q = busy.setdefault(o["e"], [])
                k = 0
                for k0, (u, v) in enumerate(q):
                    if v <= s:
                        k = k0 + 1
                    elif u >= s + o["c"]:
                        break
                    else:
                        s, k = v, k0 + 1
                q.insert(k, (s, s + o["c"]))
            start[i], fin[i] = s, s + o["c"] + o["l"]
            for k in succ[i]:
                left[k] -= 1
                if left[k] == 0:
                    ready.append((-p[k], k))
        return start, fin

    rng = np.random.default_rng(0)
    start, fin = place(pr)
    for _ in range(TRIES):
        p = pr + rng.normal(0, 1000, n) * (rng.random(n) < 0.03)
        s2, f2 = place(p)
        if max(f2) <= max(fin):
            pr, start, fin = p, s2, f2
    order = sorted(range(n), key=lambda i: (start[i], i))
    count, tick, known, clock, waits = {}, {}, {}, {}, {}
    for i in order:
        o = ops[i]
        kn = known.setdefault(o["e"], {})
        ws = {}
        if o["e"] != "N":
            for j, w in dep[i].items():
                if w and ops[j]["s"] != "sent":
                    s, v = tick[j]
                    ws[s] = max(ws.get(s, (0, j)), (v, j))
            out = []
            for s, (v, j) in sorted(ws.items(), key=lambda x: -fin[x[1][1]]):
                if kn.get(s, 0) < v:
                    out.append((s, v))
                    for s2, v2 in clock[j].items():
                        kn[s2] = max(kn.get(s2, 0), v2)
            waits[i] = out
        if o["s"] is None:
            count[o["e"]] = count.get(o["e"], 0) + 1
            tick[i] = (o["e"], count[o["e"]])
        else:
            tick[i] = (o["s"], 1)
        clock[i] = dict(kn) if o["e"] != "N" else {}
        clock[i][tick[i][0]] = tick[i][1]
    return order, waits, count, max(fin), start, fin, pr


CACHE = {}


def bits(m):
    return bin(m).count("1")


def way(T, topo, rank, name):
    t, b = int(name[2]), int(name[3])
    src, dst = T.cores[rank], T.cores[(rank + 1 + t % (len(T.cores) - 1)) % len(T.cores)]
    if topo.may_write(src, dst):
        return src, None, dst
    hs = [h for h in topo.cores_of(src) if T.rank_of(h) is None and topo.may_write(h, dst)]
    hs.sort(key=lambda h: (topo.die(h) != topo.die(src)) != (name[1] == "Y"))
    return src, hs[b % len(hs)], dst


def piece(T, name):
    if name[1] == "Y":
        return T["win" + name[2:]][:, 136:272]
    if name[1] == "K":
        return T["land" + name[2:]][:, 0:4]
    return T["land" + name[2:]][:, (4 if name[2] == "0" else 0):68]


def rank_program(g, core, T, topo):
    rank = T.rank_of(core)
    N = len(T.cores)
    if rank is None:
        sent = 0
        for t in range(RO):
            for b in range(NB):
                for name in ["%s%d%d" % (k, t, b) for k in (("aK", "aY", "aE") if t == 0 else ("aY", "aE"))]:
                    for r in range(N):
                        src, h, dst = way(T, topo, r, name)
                        if h == core:
                            rid, pid = topo.addr(dst, core)
                            m = topo.mask(core, dst)
                            g.wait_ge(T.sem[name], bits(topo.mask(src, core)))
                            g.remote_dma(piece(T, name), piece(T, name), T.sem[name], T.sem.sent, pid, rid, m)
                            sent += bits(m)
        if sent:
            g.wait_ge(T.sem.sent, sent)
        return
    if "p" not in CACHE:
        ops = build()
        CACHE["p"] = (ops,) + plan(ops)
    ops, order, waits, count = CACHE["p"][:4]
    sent = [0]

    def send(t, name, src_ap, dst_ap):
        src, h, dst = way(T, topo, rank, name)
        to = dst if h is None else h
        rid, pid = topo.addr(to, core)
        m = topo.mask(core, to)
        g.remote_dma(dst_ap, src_ap, T.sem[name], T.sem.sent, pid, rid, m)
        sent[0] += bits(m)

    def full(s, v):
        if s in ("V", "A", "P", "G"):
            return v
        if s[0] == "d":
            return 16
        src, h, dst = way(T, topo, (rank - 1 - int(s[2]) % (N - 1)) % N, s)
        return bits(topo.mask(src if h is None else h, dst))

    ctx = {"send": send}
    queue = {"V": g.vector, "A": g.scalar, "P": g.tensor, "G": g, "S": g.sync}
    for i in order:
        o = ops[i]
        if o["e"] == "N":
            continue
        for s, v in waits[i]:
            queue[o["e"]].wait_ge(T.sem[s], full(s, v))
        x = o["f"](g, T, ctx)
        if o["s"] is None:
            x.then_inc(T.sem[o["e"]], 1)
        elif o["s"] != "sent":
            x.then_inc(T.sem[o["s"]], 16)
    for e in ("V", "A", "P", "G"):
        g.wait_ge(T.sem[e], count[e])
    g.wait_ge(T.sem.sent, sent[0])
    for s in ("d_ys", "d_yn", "d_ya"):
        g.wait_ge(T.sem[s], 16)
